import numpy as np
CORES = [36,164,52,180,100,228,116,244]
N = 8
F = 128
BETA, LR = 0.75, 0.5
def setup_inputs(rng):
    return {"gr": rng.standard_normal((N, 128, N * F), dtype=np.float32), "m": rng.standard_normal((N, 128, F), dtype=np.float32), "w": rng.standard_normal((N, 128, F), dtype=np.float32)}
def setup_inputs_big(rng):
    d = setup_inputs(rng)
    for k in ("gr", "m", "w"): d[k] = (d[k].astype(np.float32) * 1048576.0).astype(d[k].dtype)
    return d
def setup_inputs_small(rng):
    d = setup_inputs(rng)
    for k in ("gr", "m", "w"): d[k] = (d[k].astype(np.float32) * (1 / 1048576.0)).astype(d[k].dtype)
    return d
def setup_inputs_apart(rng):
    d = setup_inputs(rng)
    f = (10.0 ** rng.permutation(np.linspace(-1.5, 1.5, N))).astype(np.float32).reshape(N, 1, 1)
    for k in ("gr", "m", "w"): d[k] = (d[k].astype(np.float32) * f).astype(d[k].dtype)
    return d
def reference(gr, m, w):
    GR, M, W = gr.astype(np.float64), m.astype(np.float64), w.astype(np.float64)
    s = GR.sum(axis=0)
    m2 = np.stack([BETA * M[r] + s[:, F * r:F * r + F] for r in range(N)])
    w2 = np.concatenate([W[r] - LR * m2[r] for r in range(N)], axis=1)
    return {"y": np.broadcast_to(w2.astype(np.float32), (N, 128, N * F)), "mo": m2.astype(np.float32)}

@@ -1,0 +1,135 @@
+from concourse.bass import DstId, RemoteDMATransfer
+from concourse.mybir import AluOpType
+
+N, F = 8, 128
+BETA, LR = 0.75, 0.5
+
+SCRATCH = {
+    "G": ("sbuf", [128, N * F], "float32"),
+    "SA": ("sbuf", [128, 4 * F], "float32"),
+    "SC": ("sbuf", [128, 2 * F], "float32"),
+    "L": ("sbuf", [128, 7 * F], "float32"),
+    "Y": ("sbuf", [128, N * F], "float32"),
+    "M": ("sbuf", [128, F], "float32"),
+    "W": ("sbuf", [128, F], "float32"),
+    "A": ("sbuf", [128, F], "float32"),
+    "B": ("sbuf", [128, F], "float32"),
+    "Q0": ("sbuf", [128, F], "float32"),
+    "D": ("sbuf", [128, F], "float32"),
+    "MO": ("sbuf", [128, F], "float32"),
+    "CH": ("sbuf", [128, 4 * F], "float32"),
+    "CM": ("sbuf", [128, F], "float32"),
+    "P": ("psum", [128, 4 * F], "float32"),
+}
+SEMAPHORES = ["ldA", "ldB", "ldC", "ldM", "ldW", "vmem", "vq", "scA", "scC", "wdone", "mdone",
+              "rsa", "rsb", "rsc", "aga", "agb", "agc", "sent", "stH", "stQ", "stL", "stM"]
+
+
+def cols(b, n=1):
+    return slice(b * F, (b + n) * F)
+
+
+def bits(engines):
+    m = 0
+    for e in engines:
+        m |= 1 << e
+    return m
+
+
+def rank_program(g, core, T, topo):
+    r = T.rank_of(core)
+    if r is None:
+        return
+    sem, v = T.sem, g.vector
+    half, pair, mine = (r ^ 4) & ~3, (r ^ 2) & ~1, r & ~1
+
+    common = topo.mask(core, T.cores[r ^ 1])
+    for k in range(2, N):
+        common &= topo.mask(core, T.cores[r ^ k])
+    eng = [e for e in range(common.bit_length()) if (common >> e) & 1]
+    sent = [0]
+
+    def stage(ks, src_of, dst_of, remote_sem):
+        n = len(eng) // len(ks)
+        trs = []
+        for i, k in enumerate(ks):
+            rid, pid = topo.addr(T.cores[r ^ k], core)
+            trs.append(RemoteDMATransfer(dst_ids=[DstId(rid=rid, pnc=pid)], dma_engine_mask=bits(eng[i * n:(i + 1) * n]),
+                                         remote_sem=remote_sem, src=src_of(k), dst=dst_of(k)))
+            sent[0] += n
+        g.remote_dma_fused(trs, local_sem=sem.sent)
+
+    g.sync.dma_start(out=T.G[:, cols(pair, 2)], in_=T.gr[:, cols(pair, 2)]).then_inc(sem.ldB, 16)
+    g.sync.dma_start(out=T.G[:, cols(half, 4)], in_=T.gr[:, cols(half, 4)]).then_inc(sem.ldA, 16)
+    g.sync.dma_start(out=T.G[:, cols(mine, 2)], in_=T.gr[:, cols(mine, 2)]).then_inc(sem.ldC, 16)
+    g.sync.dma_start(out=T.M[:], in_=T.m[:]).then_inc(sem.ldM, 16)
+    g.sync.dma_start(out=T.W[:], in_=T.w[:]).then_inc(sem.ldW, 16)
+
+    land = lambda k: T.L[:, cols(k - 1)]
+    g.wait_ge(sem.ldB, 16)
+    stage((2, 3), lambda k: T.G[:, cols(r ^ k)], land, sem.rsa)
+    g.wait_ge(sem.scA, 1)
+    stage((4, 5, 6, 7), lambda k: T.SA[:, cols((r ^ k) - half)], land, sem.rsb)
+    g.wait_ge(sem.scC, 1)
+    stage((1,), lambda k: T.SC[:, cols((r ^ k) - mine)], land, sem.rsc)
+    own = lambda k: T.Y[:, cols(r)]
+    g.wait_ge(sem.wdone, 1)
+    stage((4, 5, 6, 7), own, own, sem.aga)
+    stage((2, 3), own, own, sem.agb)
+    stage((1,), own, own, sem.agc)
+
+    nq = [0]
+
+    def tt(out, a, b, op, done=None):
+        if nq[0]:
+            v.wait_ge(sem.vq, nq[0])
+        ins = v.tensor_tensor(out, a, b, op)
+        if done is None:
+            ins.then_inc(sem.vq, 1)
+            nq[0] += 1
+        else:
+            ins.then_inc(done, 1)
+
+    add, sub, mul = AluOpType.add, AluOpType.subtract, AluOpType.mult
+    v.memset(T.CH[:], -LR).then_inc(sem.vmem, 1)
+    v.memset(T.CM[:], -LR * BETA).then_inc(sem.vmem, 1)
+    v.wait_ge(sem.vmem, 2)
+    v.wait_ge(sem.ldA, 16)
+    tt(T.SA[:], T.G[:, cols(half, 4)], T.CH[:], mul, sem.scA)
+    v.wait_ge(sem.ldC, 16)
+    tt(T.SC[:], T.G[:, cols(mine, 2)], T.CH[:, cols(0, 2)], mul, sem.scC)
+    v.wait_ge(sem.ldM, 16)
+    tt(T.A[:], T.M[:], T.CM[:], mul)
+    v.wait_ge(sem.ldW, 16)
+    tt(T.B[:], T.W[:], T.A[:], add)
+    v.wait_ge(sem.scC, 1)
+    tt(T.Q0[:], T.B[:], T.SC[:, cols(r - mine)], add)
+    U, H, Q = T.P[:, cols(0)], T.P[:, cols(1)], T.P[:, cols(2)]
+    v.wait_ge(sem.rsa, len(eng))
+    tt(U, land(2), land(3), add)
+    tt(H, U, T.CH[:, cols(0)], mul)
+    tt(Q, H, T.Q0[:], add)
+    v.wait_ge(sem.rsb, len(eng))
+    for k in (4, 5, 6, 7):
+        tt(Q, Q, land(k), add)
+    v.wait_ge(sem.rsc, len(eng))
+    tt(T.Y[:, cols(r)], Q, land(1), add, sem.wdone)
+    v.wait_ge(sem.wdone, 1)
+    tt(T.D[:], T.W[:], T.Y[:, cols(r)], sub)
+    tt(T.MO[:], T.D[:], T.D[:], add, sem.mdone)
+
+    g.scalar.wait_ge(sem.aga, len(eng))
+    g.scalar.dma_start(out=T.y[:, cols(half, 4)], in_=T.Y[:, cols(half, 4)]).then_inc(sem.stH, 16)
+    g.scalar.wait_ge(sem.mdone, 1)
+    g.scalar.dma_start(out=T.mo[:], in_=T.MO[:]).then_inc(sem.stM, 16)
+    g.sync.wait_ge(sem.agb, len(eng))
+    g.sync.dma_start(out=T.y[:, cols(pair, 2)], in_=T.Y[:, cols(pair, 2)]).then_inc(sem.stQ, 16)
+    g.sync.wait_ge(sem.wdone, 1)
+    g.sync.wait_ge(sem.agc, len(eng))
+    g.sync.dma_start(out=T.y[:, cols(mine, 2)], in_=T.Y[:, cols(mine, 2)]).then_inc(sem.stL, 16)
+
+    g.wait_ge(sem.sent, sent[0])
+    g.scalar.wait_ge(sem.stH, 16)
+    g.scalar.wait_ge(sem.stM, 16)
+    g.sync.wait_ge(sem.stQ, 16)
+    g.sync.wait_ge(sem.stL, 16)

@@ -2,27 +2,34 @@ from concourse.bass import DstId, RemoteDMATransfer
 from concourse.mybir import AluOpType
 
 N, F = 8, 128
+QW = 32
 BETA, LR = 0.75, 0.5
+WORLD = 256
 
 SCRATCH = {
     "G": ("sbuf", [128, N * F], "float32"),
-    "SA": ("sbuf", [128, 4 * F], "float32"),
-    "SC": ("sbuf", [128, 2 * F], "float32"),
+    "S": ("sbuf", [128, 6 * F], "float32"),
+    "SO": ("sbuf", [128, F], "float32"),
     "L": ("sbuf", [128, 7 * F], "float32"),
+    "LX": ("sbuf", [128, QW], "float32"),
+    "HX": ("sbuf", [128, QW], "float32"),
     "Y": ("sbuf", [128, N * F], "float32"),
     "M": ("sbuf", [128, F], "float32"),
     "W": ("sbuf", [128, F], "float32"),
-    "A": ("sbuf", [128, F], "float32"),
-    "B": ("sbuf", [128, F], "float32"),
-    "Q0": ("sbuf", [128, F], "float32"),
-    "D": ("sbuf", [128, F], "float32"),
+    "Z0": ("sbuf", [128, F], "float32"),
+    "Z1": ("sbuf", [128, F], "float32"),
+    "T3": ("sbuf", [128, 3 * F], "float32"),
     "MO": ("sbuf", [128, F], "float32"),
-    "CH": ("sbuf", [128, 4 * F], "float32"),
+    "CH": ("sbuf", [128, 2 * F], "float32"),
     "CM": ("sbuf", [128, F], "float32"),
+    "C2": ("sbuf", [128, F], "float32"),
+    "X0": ("sbuf", [128, QW], "float32"),
+    "XW": ("sbuf", [128, F], "float32"),
     "P": ("psum", [128, 4 * F], "float32"),
 }
-SEMAPHORES = ["ldA", "ldB", "ldC", "ldM", "ldW", "vmem", "vq", "scA", "scC", "wdone", "mdone",
-              "rsa", "rsb", "rsc", "aga", "agb", "agc", "sent", "stH", "stQ", "stL", "stM"]
+SEMAPHORES = ["ld0", "ld1", "ld2", "ld3", "ldO", "ldM", "ldW", "vmem", "vq", "sc2", "sc3", "sc4", "wdone", "mdone",
+              "xb", "xw", "rsx", "rs1", "rsa", "rsb", "rsd", "rse", "aga", "agb", "agd", "agc", "sent",
+              "stH", "stQ", "stR", "stL", "stO", "stM"]
 
 
 def cols(b, n=1):
@@ -36,47 +43,98 @@ def bits(engines):
     return m
 
 
-def rank_program(g, core, T, topo):
-    r = T.rank_of(core)
-    if r is None:
-        return
-    sem, v = T.sem, g.vector
-    half, pair, mine = (r ^ 4) & ~3, (r ^ 2) & ~1, r & ~1
+def engines_of(mask):
+    return [e for e in range(mask.bit_length()) if (mask >> e) & 1]
 
-    common = topo.mask(core, T.cores[r ^ 1])
+
+def helper_of(R, T, topo):
+    for c in range(WORLD):
+        if (T.rank_of(c) is None and topo.host(c) == topo.host(R) and topo.chip(c) == topo.chip(R)
+                and topo.die(c) != topo.die(R) and all(topo.may_write(c, p) for p in T.cores if p != R)):
+            return c
+    return None
+
+
+def off_chip(src, T, topo, r):
+    common = topo.mask(src, T.cores[r ^ 1])
     for k in range(2, N):
-        common &= topo.mask(core, T.cores[r ^ k])
-    eng = [e for e in range(common.bit_length()) if (common >> e) & 1]
+        common &= topo.mask(src, T.cores[r ^ k])
+    return common
+
+
+def rank_program(g, core, T, topo):
+    sem = T.sem
     sent = [0]
 
-    def stage(ks, src_of, dst_of, remote_sem):
-        n = len(eng) // len(ks)
+    def send(items):
         trs = []
-        for i, k in enumerate(ks):
-            rid, pid = topo.addr(T.cores[r ^ k], core)
-            trs.append(RemoteDMATransfer(dst_ids=[DstId(rid=rid, pnc=pid)], dma_engine_mask=bits(eng[i * n:(i + 1) * n]),
-                                         remote_sem=remote_sem, src=src_of(k), dst=dst_of(k)))
-            sent[0] += n
+        for dst_core, engs, src, dst, rsem in items:
+            rid, pid = topo.addr(dst_core, core)
+            trs.append(RemoteDMATransfer(dst_ids=[DstId(rid=rid, pnc=pid)], dma_engine_mask=bits(engs),
+                                         remote_sem=rsem, src=src, dst=dst))
+            sent[0] += len(engs)
         g.remote_dma_fused(trs, local_sem=sem.sent)
 
-    g.sync.dma_start(out=T.G[:, cols(pair, 2)], in_=T.gr[:, cols(pair, 2)]).then_inc(sem.ldB, 16)
-    g.sync.dma_start(out=T.G[:, cols(half, 4)], in_=T.gr[:, cols(half, 4)]).then_inc(sem.ldA, 16)
-    g.sync.dma_start(out=T.G[:, cols(mine, 2)], in_=T.gr[:, cols(mine, 2)]).then_inc(sem.ldC, 16)
+    r = T.rank_of(core)
+
+    if r is None:
+        for i in range(N):
+            if helper_of(T.cores[i], T, topo) == core:
+                r = i
+        if r is None:
+            return
+        R = T.cores[r]
+        nup = len(engines_of(topo.mask(R, core) & ~off_chip(R, T, topo, r)))
+        xe = engines_of(topo.mask(core, T.cores[r ^ 1]))
+        g.wait_ge(sem.xb, nup)
+        send([(T.cores[r ^ 1], xe, T.X0[:], T.LX[:], sem.rsx)])
+        g.wait_ge(sem.xw, nup)
+        send([(T.cores[r ^ 1], xe, T.XW[:], T.Y[:, cols(r)], sem.agc)])
+        g.wait_ge(sem.sent, sent[0])
+        return
+
+    v = g.vector
+    X = helper_of(core, T, topo)
+    half = (r ^ 4) & ~3
+    first = {2: (r ^ 2) & ~1, 4: (r ^ 4) & ~1, 6: (r ^ 6) & ~1}
+    off = off_chip(core, T, topo, r)
+    eng = engines_of(off)
+    up = engines_of(topo.mask(core, X) & ~off)
+    ne = len(eng)
+    nx = len(engines_of(topo.mask(X, T.cores[r ^ 1])))
+    c0 = (r ^ 1) * F
+
+    def stage(ks, src_of, dst_of, remote_sem, more=()):
+        n = ne // len(ks)
+        send(list(more) + [(T.cores[r ^ k], eng[i * n:(i + 1) * n], src_of(k), dst_of(k), remote_sem)
+                           for i, k in enumerate(ks)])
+
+    g.sync.dma_start(out=T.G[:, c0:c0 + QW], in_=T.gr[:, c0:c0 + QW]).then_inc(sem.ld0, 16)
+    g.sync.dma_start(out=T.G[:, c0 + QW:c0 + F], in_=T.gr[:, c0 + QW:c0 + F]).then_inc(sem.ld1, 16)
+    g.sync.dma_start(out=T.G[:, cols(first[2], 2)], in_=T.gr[:, cols(first[2], 2)]).then_inc(sem.ld2, 16)
+    g.sync.dma_start(out=T.G[:, cols(half, 4)], in_=T.gr[:, cols(half, 4)]).then_inc(sem.ld3, 16)
+    g.sync.dma_start(out=T.G[:, cols(r)], in_=T.gr[:, cols(r)]).then_inc(sem.ldO, 16)
     g.sync.dma_start(out=T.M[:], in_=T.m[:]).then_inc(sem.ldM, 16)
     g.sync.dma_start(out=T.W[:], in_=T.w[:]).then_inc(sem.ldW, 16)
 
     land = lambda k: T.L[:, cols(k - 1)]
-    g.wait_ge(sem.ldB, 16)
-    stage((2, 3), lambda k: T.G[:, cols(r ^ k)], land, sem.rsa)
-    g.wait_ge(sem.scA, 1)
-    stage((4, 5, 6, 7), lambda k: T.SA[:, cols((r ^ k) - half)], land, sem.rsb)
-    g.wait_ge(sem.scC, 1)
-    stage((1,), lambda k: T.SC[:, cols((r ^ k) - mine)], land, sem.rsc)
+    scaled = lambda k: T.S[:, cols((k & ~1) - 2 + (r ^ k) - first[k & ~1])]
     own = lambda k: T.Y[:, cols(r)]
+    g.wait_ge(sem.ld0, 16)
+    send([(X, up, T.G[:, c0:c0 + QW], T.X0[:], sem.xb)])
+    g.wait_ge(sem.ld1, 16)
+    send([(T.cores[r ^ 1], eng, T.G[:, c0 + QW:c0 + F], T.L[:, QW:F], sem.rs1)])
+    g.wait_ge(sem.sc2, 1)
+    stage((2, 3), scaled, land, sem.rsa)
+    g.wait_ge(sem.sc3, 1)
+    stage((4, 5), scaled, land, sem.rsb)
+    g.wait_ge(sem.sc4, 1)
+    stage((6,), scaled, land, sem.rsd)
+    stage((7,), scaled, land, sem.rse)
     g.wait_ge(sem.wdone, 1)
-    stage((4, 5, 6, 7), own, own, sem.aga)
-    stage((2, 3), own, own, sem.agb)
-    stage((1,), own, own, sem.agc)
+    stage((4, 5, 6, 7), own, own, sem.aga, more=[(X, up, own(0), T.XW[:], sem.xw)])
+    stage((2,), own, own, sem.agb)
+    stage((3,), own, own, sem.agd)
 
     nq = [0]
 
@@ -90,46 +148,63 @@ def rank_program(g, core, T, topo):
         else:
             ins.then_inc(done, 1)
 
-    add, sub, mul = AluOpType.add, AluOpType.subtract, AluOpType.mult
+    add, mul = AluOpType.add, AluOpType.mult
+    A, H1, Q, U = T.P[:, cols(0)], T.P[:, cols(1)], T.P[:, cols(2)], T.P[:, cols(3)]
+    Qq, Uq = T.P[:, 2 * F:2 * F + QW], T.P[:, 3 * F:3 * F + QW]
+    ch1 = T.CH[:, cols(0)]
     v.memset(T.CH[:], -LR).then_inc(sem.vmem, 1)
     v.memset(T.CM[:], -LR * BETA).then_inc(sem.vmem, 1)
-    v.wait_ge(sem.vmem, 2)
-    v.wait_ge(sem.ldA, 16)
-    tt(T.SA[:], T.G[:, cols(half, 4)], T.CH[:], mul, sem.scA)
-    v.wait_ge(sem.ldC, 16)
-    tt(T.SC[:], T.G[:, cols(mine, 2)], T.CH[:, cols(0, 2)], mul, sem.scC)
+    v.memset(T.C2[:], -1.0 / LR).then_inc(sem.vmem, 1)
+    v.memset(T.L[:, 0:QW], 0.0).then_inc(sem.vmem, 1)
+    v.wait_ge(sem.vmem, 4)
+    v.wait_ge(sem.ld2, 16)
+    tt(T.S[:, cols(0, 2)], T.G[:, cols(first[2], 2)], T.CH[:], mul, sem.sc2)
+    v.wait_ge(sem.ld3, 16)
+    tt(T.S[:, cols(2, 2)], T.G[:, cols(first[4], 2)], T.CH[:], mul, sem.sc3)
+    tt(T.S[:, cols(4, 2)], T.G[:, cols(first[6], 2)], T.CH[:], mul, sem.sc4)
+    v.wait_ge(sem.ldO, 16)
+    tt(T.SO[:], T.G[:, cols(r)], ch1, mul)
     v.wait_ge(sem.ldM, 16)
-    tt(T.A[:], T.M[:], T.CM[:], mul)
+    tt(A, T.M[:], T.CM[:], mul)
+    tt(T.Z0[:], A, T.SO[:], add)
+    v.wait_ge(sem.rs1, ne)
+    tt(H1, land(1), ch1, mul)
+    tt(T.Z1[:], H1, T.Z0[:], add)
     v.wait_ge(sem.ldW, 16)
-    tt(T.B[:], T.W[:], T.A[:], add)
-    v.wait_ge(sem.scC, 1)
-    tt(T.Q0[:], T.B[:], T.SC[:, cols(r - mine)], add)
-    U, H, Q = T.P[:, cols(0)], T.P[:, cols(1)], T.P[:, cols(2)]
-    v.wait_ge(sem.rsa, len(eng))
-    tt(U, land(2), land(3), add)
-    tt(H, U, T.CH[:, cols(0)], mul)
-    tt(Q, H, T.Q0[:], add)
-    v.wait_ge(sem.rsb, len(eng))
-    for k in (4, 5, 6, 7):
-        tt(Q, Q, land(k), add)
-    v.wait_ge(sem.rsc, len(eng))
-    tt(T.Y[:, cols(r)], Q, land(1), add, sem.wdone)
-    v.wait_ge(sem.wdone, 1)
-    tt(T.D[:], T.W[:], T.Y[:, cols(r)], sub)
-    tt(T.MO[:], T.D[:], T.D[:], add, sem.mdone)
+    tt(Q, T.Z1[:], T.W[:], add)
+    for s, ks in ((sem.rsa, (2, 3)), (sem.rsb, (4, 5)), (sem.rsd, (6,))):
+        v.wait_ge(s, ne)
+        for k in ks:
+            tt(Q, Q, land(k), add)
+    v.wait_ge(sem.rsx, nx)
+    tt(T.HX[:], T.LX[:], T.CH[:, 0:QW], mul)
+    tt(Qq, Qq, T.HX[:], add)
+    v.wait_ge(sem.rse, ne)
+    tt(T.Y[:, cols(r)], Q, land(7), add, sem.wdone)
+    tt(T.T3[:], T.L[:, cols(1, 3)], T.L[:, cols(4, 3)], add)
+    tt(U, T.T3[:, cols(0)], T.T3[:, cols(1)], add)
+    tt(U, U, T.T3[:, cols(2)], add)
+    tt(U, U, T.Z1[:], add)
+    tt(Uq, Uq, T.HX[:], add)
+    tt(T.MO[:], U, T.C2[:], mul, sem.mdone)
 
-    g.scalar.wait_ge(sem.aga, len(eng))
+    g.scalar.wait_ge(sem.aga, ne)
     g.scalar.dma_start(out=T.y[:, cols(half, 4)], in_=T.Y[:, cols(half, 4)]).then_inc(sem.stH, 16)
+    g.scalar.wait_ge(sem.wdone, 1)
+    g.scalar.dma_start(out=T.y[:, cols(r)], in_=T.Y[:, cols(r)]).then_inc(sem.stO, 16)
     g.scalar.wait_ge(sem.mdone, 1)
     g.scalar.dma_start(out=T.mo[:], in_=T.MO[:]).then_inc(sem.stM, 16)
-    g.sync.wait_ge(sem.agb, len(eng))
-    g.sync.dma_start(out=T.y[:, cols(pair, 2)], in_=T.Y[:, cols(pair, 2)]).then_inc(sem.stQ, 16)
-    g.sync.wait_ge(sem.wdone, 1)
-    g.sync.wait_ge(sem.agc, len(eng))
-    g.sync.dma_start(out=T.y[:, cols(mine, 2)], in_=T.Y[:, cols(mine, 2)]).then_inc(sem.stL, 16)
+    g.scalar.wait_ge(sem.agc, nx)
+    g.scalar.dma_start(out=T.y[:, cols(r ^ 1)], in_=T.Y[:, cols(r ^ 1)]).then_inc(sem.stL, 16)
+    g.sync.wait_ge(sem.agb, ne)
+    g.sync.dma_start(out=T.y[:, cols(r ^ 2)], in_=T.Y[:, cols(r ^ 2)]).then_inc(sem.stQ, 16)
+    g.sync.wait_ge(sem.agd, ne)
+    g.sync.dma_start(out=T.y[:, cols(r ^ 3)], in_=T.Y[:, cols(r ^ 3)]).then_inc(sem.stR, 16)
 
     g.wait_ge(sem.sent, sent[0])
     g.scalar.wait_ge(sem.stH, 16)
+    g.scalar.wait_ge(sem.stO, 16)
     g.scalar.wait_ge(sem.stM, 16)
+    g.scalar.wait_ge(sem.stL, 16)
     g.sync.wait_ge(sem.stQ, 16)
-    g.sync.wait_ge(sem.stL, 16)
+    g.sync.wait_ge(sem.stR, 16)

@@ -20,16 +20,13 @@ SCRATCH = {
     "Z1": ("sbuf", [128, F], "float32"),
     "T3": ("sbuf", [128, 3 * F], "float32"),
     "MO": ("sbuf", [128, F], "float32"),
-    "CH": ("sbuf", [128, 2 * F], "float32"),
-    "CM": ("sbuf", [128, F], "float32"),
-    "C2": ("sbuf", [128, F], "float32"),
     "X0": ("sbuf", [128, QW], "float32"),
     "XW": ("sbuf", [128, F], "float32"),
     "P": ("psum", [128, 4 * F], "float32"),
 }
 SEMAPHORES = ["ld0", "ld1", "ld2", "ld3", "ldO", "ldM", "ldW", "vmem", "vq", "sc2", "sc3", "sc4", "wdone", "mdone",
-              "xb", "xw", "rsx", "rs1", "rsa", "rsb", "rsd", "rse", "aga", "agb", "agd", "agc", "sent",
-              "stH", "stQ", "stR", "stL", "stO", "stM"]
+              "xb", "xw", "rsx", "rs1", "rsa", "rsb", "rsd", "rse", "aga", "agp", "agb", "agd", "agc", "agi", "sent",
+              "stH", "stP", "stQ", "stR", "stL", "stO", "stM"]
 
 
 def cols(b, n=1):
@@ -85,11 +82,12 @@ def rank_program(g, core, T, topo):
             return
         R = T.cores[r]
         nup = len(engines_of(topo.mask(R, core) & ~off_chip(R, T, topo, r)))
-        xe = engines_of(topo.mask(core, T.cores[r ^ 1]))
+        xe = engines_of(off_chip(core, T, topo, r))
         g.wait_ge(sem.xb, nup)
         send([(T.cores[r ^ 1], xe, T.X0[:], T.LX[:], sem.rsx)])
         g.wait_ge(sem.xw, nup)
         send([(T.cores[r ^ 1], xe, T.XW[:], T.Y[:, cols(r)], sem.agc)])
+        send([(T.cores[r ^ 3], xe, T.XW[:], T.Y[:, cols(r)], sem.agd)])
         g.wait_ge(sem.sent, sent[0])
         return
 
@@ -101,7 +99,7 @@ def rank_program(g, core, T, topo):
     eng = engines_of(off)
     up = engines_of(topo.mask(core, X) & ~off)
     ne = len(eng)
-    nx = len(engines_of(topo.mask(X, T.cores[r ^ 1])))
+    nx = len(engines_of(off_chip(X, T, topo, r)))
     c0 = (r ^ 1) * F
 
     def stage(ks, src_of, dst_of, remote_sem, more=()):
@@ -110,7 +108,7 @@ def rank_program(g, core, T, topo):
                            for i, k in enumerate(ks)])
 
     g.sync.dma_start(out=T.G[:, c0:c0 + QW], in_=T.gr[:, c0:c0 + QW]).then_inc(sem.ld0, 16)
-    g.sync.dma_start(out=T.G[:, c0 + QW:c0 + F], in_=T.gr[:, c0 + QW:c0 + F]).then_inc(sem.ld1, 16)
+    g.scalar.dma_start(out=T.G[:, c0 + QW:c0 + F], in_=T.gr[:, c0 + QW:c0 + F]).then_inc(sem.ld1, 16)
     g.sync.dma_start(out=T.G[:, cols(first[2], 2)], in_=T.gr[:, cols(first[2], 2)]).then_inc(sem.ld2, 16)
     g.sync.dma_start(out=T.G[:, cols(half, 4)], in_=T.gr[:, cols(half, 4)]).then_inc(sem.ld3, 16)
     g.sync.dma_start(out=T.G[:, cols(r)], in_=T.gr[:, cols(r)]).then_inc(sem.ldO, 16)
@@ -132,79 +130,86 @@ def rank_program(g, core, T, topo):
     stage((6,), scaled, land, sem.rsd)
     stage((7,), scaled, land, sem.rse)
     g.wait_ge(sem.wdone, 1)
-    stage((4, 5, 6, 7), own, own, sem.aga, more=[(X, up, own(0), T.XW[:], sem.xw)])
+    stage((4, 5), own, own, sem.aga, more=[(X, up, own(0), T.XW[:], sem.xw)])
+    stage((6, 7), own, own, sem.agp)
     stage((2,), own, own, sem.agb)
-    stage((3,), own, own, sem.agd)
+    g.sem_inc(sem.agi, 1)
 
     nq = [0]
+    add, mul = AluOpType.add, AluOpType.mult
 
-    def tt(out, a, b, op, done=None):
+    def after(make, done):
         if nq[0]:
             v.wait_ge(sem.vq, nq[0])
-        ins = v.tensor_tensor(out, a, b, op)
+        ins = make()
         if done is None:
             ins.then_inc(sem.vq, 1)
             nq[0] += 1
         else:
             ins.then_inc(done, 1)
 
-    add, mul = AluOpType.add, AluOpType.mult
+    def tt(out, a, b, done=None):
+        after(lambda: v.tensor_tensor(out, a, b, add), done)
+
+    def ts(out, a, c, done=None):
+        after(lambda: v.tensor_scalar(out, a, c, None, mul), done)
+
     A, H1, Q, U = T.P[:, cols(0)], T.P[:, cols(1)], T.P[:, cols(2)], T.P[:, cols(3)]
     Qq, Uq = T.P[:, 2 * F:2 * F + QW], T.P[:, 3 * F:3 * F + QW]
-    ch1 = T.CH[:, cols(0)]
-    v.memset(T.CH[:], -LR).then_inc(sem.vmem, 1)
-    v.memset(T.CM[:], -LR * BETA).then_inc(sem.vmem, 1)
-    v.memset(T.C2[:], -1.0 / LR).then_inc(sem.vmem, 1)
     v.memset(T.L[:, 0:QW], 0.0).then_inc(sem.vmem, 1)
-    v.wait_ge(sem.vmem, 4)
+    v.wait_ge(sem.vmem, 1)
     v.wait_ge(sem.ld2, 16)
-    tt(T.S[:, cols(0, 2)], T.G[:, cols(first[2], 2)], T.CH[:], mul, sem.sc2)
+    ts(T.S[:, cols(0, 2)], T.G[:, cols(first[2], 2)], -LR, sem.sc2)
     v.wait_ge(sem.ld3, 16)
-    tt(T.S[:, cols(2, 2)], T.G[:, cols(first[4], 2)], T.CH[:], mul, sem.sc3)
-    tt(T.S[:, cols(4, 2)], T.G[:, cols(first[6], 2)], T.CH[:], mul, sem.sc4)
+    ts(T.S[:, cols(2, 2)], T.G[:, cols(first[4], 2)], -LR, sem.sc3)
+    ts(T.S[:, cols(4, 2)], T.G[:, cols(first[6], 2)], -LR, sem.sc4)
     v.wait_ge(sem.ldO, 16)
-    tt(T.SO[:], T.G[:, cols(r)], ch1, mul)
+    ts(T.SO[:], T.G[:, cols(r)], -LR)
     v.wait_ge(sem.ldM, 16)
-    tt(A, T.M[:], T.CM[:], mul)
-    tt(T.Z0[:], A, T.SO[:], add)
+    ts(A, T.M[:], -LR * BETA)
+    tt(T.Z0[:], A, T.SO[:])
     v.wait_ge(sem.rs1, ne)
-    tt(H1, land(1), ch1, mul)
-    tt(T.Z1[:], H1, T.Z0[:], add)
+    ts(H1, land(1), -LR)
+    tt(T.Z1[:], H1, T.Z0[:])
     v.wait_ge(sem.ldW, 16)
-    tt(Q, T.Z1[:], T.W[:], add)
+    tt(Q, T.Z1[:], T.W[:])
     for s, ks in ((sem.rsa, (2, 3)), (sem.rsb, (4, 5)), (sem.rsd, (6,))):
         v.wait_ge(s, ne)
         for k in ks:
-            tt(Q, Q, land(k), add)
+            tt(Q, Q, land(k))
     v.wait_ge(sem.rsx, nx)
-    tt(T.HX[:], T.LX[:], T.CH[:, 0:QW], mul)
-    tt(Qq, Qq, T.HX[:], add)
+    ts(T.HX[:], T.LX[:], -LR)
+    tt(Qq, Qq, T.HX[:])
     v.wait_ge(sem.rse, ne)
-    tt(T.Y[:, cols(r)], Q, land(7), add, sem.wdone)
-    tt(T.T3[:], T.L[:, cols(1, 3)], T.L[:, cols(4, 3)], add)
-    tt(U, T.T3[:, cols(0)], T.T3[:, cols(1)], add)
-    tt(U, U, T.T3[:, cols(2)], add)
-    tt(U, U, T.Z1[:], add)
-    tt(Uq, Uq, T.HX[:], add)
-    tt(T.MO[:], U, T.C2[:], mul, sem.mdone)
+    tt(T.Y[:, cols(r)], Q, land(7), sem.wdone)
+    tt(T.T3[:], T.L[:, cols(1, 3)], T.L[:, cols(4, 3)])
+    tt(U, T.T3[:, cols(0)], T.T3[:, cols(1)])
+    tt(U, U, T.T3[:, cols(2)])
+    tt(U, U, T.Z1[:])
+    tt(Uq, Uq, T.HX[:])
+    ts(T.MO[:], U, -1.0 / LR, sem.mdone)
 
-    g.scalar.wait_ge(sem.aga, ne)
-    g.scalar.dma_start(out=T.y[:, cols(half, 4)], in_=T.Y[:, cols(half, 4)]).then_inc(sem.stH, 16)
     g.scalar.wait_ge(sem.wdone, 1)
+    g.scalar.wait_ge(sem.agi, 1)
     g.scalar.dma_start(out=T.y[:, cols(r)], in_=T.Y[:, cols(r)]).then_inc(sem.stO, 16)
     g.scalar.wait_ge(sem.mdone, 1)
     g.scalar.dma_start(out=T.mo[:], in_=T.MO[:]).then_inc(sem.stM, 16)
     g.scalar.wait_ge(sem.agc, nx)
     g.scalar.dma_start(out=T.y[:, cols(r ^ 1)], in_=T.Y[:, cols(r ^ 1)]).then_inc(sem.stL, 16)
+    g.scalar.wait_ge(sem.agd, nx)
+    g.scalar.dma_start(out=T.y[:, cols(r ^ 3)], in_=T.Y[:, cols(r ^ 3)]).then_inc(sem.stR, 16)
+    g.sync.wait_ge(sem.aga, ne)
+    g.sync.dma_start(out=T.y[:, cols(first[4], 2)], in_=T.Y[:, cols(first[4], 2)]).then_inc(sem.stH, 16)
+    g.sync.wait_ge(sem.agp, ne)
+    g.sync.dma_start(out=T.y[:, cols(first[6], 2)], in_=T.Y[:, cols(first[6], 2)]).then_inc(sem.stP, 16)
     g.sync.wait_ge(sem.agb, ne)
     g.sync.dma_start(out=T.y[:, cols(r ^ 2)], in_=T.Y[:, cols(r ^ 2)]).then_inc(sem.stQ, 16)
-    g.sync.wait_ge(sem.agd, ne)
-    g.sync.dma_start(out=T.y[:, cols(r ^ 3)], in_=T.Y[:, cols(r ^ 3)]).then_inc(sem.stR, 16)
 
     g.wait_ge(sem.sent, sent[0])
-    g.scalar.wait_ge(sem.stH, 16)
     g.scalar.wait_ge(sem.stO, 16)
     g.scalar.wait_ge(sem.stM, 16)
     g.scalar.wait_ge(sem.stL, 16)
+    g.scalar.wait_ge(sem.stR, 16)
+    g.sync.wait_ge(sem.stH, 16)
+    g.sync.wait_ge(sem.stP, 16)
     g.sync.wait_ge(sem.stQ, 16)
-    g.sync.wait_ge(sem.stR, 16)

from concourse.bass import DstId, RemoteDMATransfer
from concourse.mybir import AluOpType

N, F = 8, 128
QW = 32
BETA, LR = 0.75, 0.5
WORLD = 256

SCRATCH = {
    "G": ("sbuf", [128, N * F], "float32"),
    "S": ("sbuf", [128, 6 * F], "float32"),
    "SO": ("sbuf", [128, F], "float32"),
    "L": ("sbuf", [128, 7 * F], "float32"),
    "LX": ("sbuf", [128, QW], "float32"),
    "HX": ("sbuf", [128, QW], "float32"),
    "Y": ("sbuf", [128, N * F], "float32"),
    "M": ("sbuf", [128, F], "float32"),
    "W": ("sbuf", [128, F], "float32"),
    "Z0": ("sbuf", [128, F], "float32"),
    "Z1": ("sbuf", [128, F], "float32"),
    "T3": ("sbuf", [128, 3 * F], "float32"),
    "MO": ("sbuf", [128, F], "float32"),
    "X0": ("sbuf", [128, QW], "float32"),
    "XW": ("sbuf", [128, F], "float32"),
    "P": ("psum", [128, 4 * F], "float32"),
}
SEMAPHORES = ["ld0", "ld1", "ld2", "ld3", "ldO", "ldM", "ldW", "vmem", "vq", "sc2", "sc3", "sc4", "wdone", "mdone",
              "xb", "xw", "rsx", "rs1", "rsa", "rsb", "rsd", "rse", "aga", "agp", "agb", "agd", "agc", "agi", "sent",
              "stH", "stP", "stQ", "stR", "stL", "stO", "stM"]


def cols(b, n=1):
    return slice(b * F, (b + n) * F)


def bits(engines):
    m = 0
    for e in engines:
        m |= 1 << e
    return m


def engines_of(mask):
    return [e for e in range(mask.bit_length()) if (mask >> e) & 1]


def helper_of(R, T, topo):
    for c in range(WORLD):
        if (T.rank_of(c) is None and topo.host(c) == topo.host(R) and topo.chip(c) == topo.chip(R)
                and topo.die(c) != topo.die(R) and all(topo.may_write(c, p) for p in T.cores if p != R)):
            return c
    return None


def off_chip(src, T, topo, r):
    common = topo.mask(src, T.cores[r ^ 1])
    for k in range(2, N):
        common &= topo.mask(src, T.cores[r ^ k])
    return common


def rank_program(g, core, T, topo):
    sem = T.sem
    sent = [0]

    def send(items):
        trs = []
        for dst_core, engs, src, dst, rsem in items:
            rid, pid = topo.addr(dst_core, core)
            trs.append(RemoteDMATransfer(dst_ids=[DstId(rid=rid, pnc=pid)], dma_engine_mask=bits(engs),
                                         remote_sem=rsem, src=src, dst=dst))
            sent[0] += len(engs)
        g.remote_dma_fused(trs, local_sem=sem.sent)

    r = T.rank_of(core)

    if r is None:
        for i in range(N):
            if helper_of(T.cores[i], T, topo) == core:
                r = i
        if r is None:
            return
        R = T.cores[r]
        nup = len(engines_of(topo.mask(R, core) & ~off_chip(R, T, topo, r)))
        xe = engines_of(off_chip(core, T, topo, r))
        g.wait_ge(sem.xb, nup)
        send([(T.cores[r ^ 1], xe, T.X0[:], T.LX[:], sem.rsx)])
        g.wait_ge(sem.xw, nup)
        send([(T.cores[r ^ 1], xe, T.XW[:], T.Y[:, cols(r)], sem.agc)])
        send([(T.cores[r ^ 3], xe, T.XW[:], T.Y[:, cols(r)], sem.agd)])
        g.wait_ge(sem.sent, sent[0])
        return

    v = g.vector
    X = helper_of(core, T, topo)
    half = (r ^ 4) & ~3
    first = {2: (r ^ 2) & ~1, 4: (r ^ 4) & ~1, 6: (r ^ 6) & ~1}
    off = off_chip(core, T, topo, r)
    eng = engines_of(off)
    up = engines_of(topo.mask(core, X) & ~off)
    ne = len(eng)
    nx = len(engines_of(off_chip(X, T, topo, r)))
    c0 = (r ^ 1) * F

    def stage(ks, src_of, dst_of, remote_sem, more=()):
        n = ne // len(ks)
        send(list(more) + [(T.cores[r ^ k], eng[i * n:(i + 1) * n], src_of(k), dst_of(k), remote_sem)
                           for i, k in enumerate(ks)])

    g.sync.dma_start(out=T.G[:, c0:c0 + QW], in_=T.gr[:, c0:c0 + QW]).then_inc(sem.ld0, 16)
    g.scalar.dma_start(out=T.G[:, c0 + QW:c0 + F], in_=T.gr[:, c0 + QW:c0 + F]).then_inc(sem.ld1, 16)
    g.sync.dma_start(out=T.G[:, cols(first[2], 2)], in_=T.gr[:, cols(first[2], 2)]).then_inc(sem.ld2, 16)
    g.sync.dma_start(out=T.G[:, cols(half, 4)], in_=T.gr[:, cols(half, 4)]).then_inc(sem.ld3, 16)
    g.sync.dma_start(out=T.G[:, cols(r)], in_=T.gr[:, cols(r)]).then_inc(sem.ldO, 16)
    g.sync.dma_start(out=T.M[:], in_=T.m[:]).then_inc(sem.ldM, 16)
    g.sync.dma_start(out=T.W[:], in_=T.w[:]).then_inc(sem.ldW, 16)

    land = lambda k: T.L[:, cols(k - 1)]
    scaled = lambda k: T.S[:, cols((k & ~1) - 2 + (r ^ k) - first[k & ~1])]
    own = lambda k: T.Y[:, cols(r)]
    g.wait_ge(sem.ld0, 16)
    send([(X, up, T.G[:, c0:c0 + QW], T.X0[:], sem.xb)])
    g.wait_ge(sem.ld1, 16)
    send([(T.cores[r ^ 1], eng, T.G[:, c0 + QW:c0 + F], T.L[:, QW:F], sem.rs1)])
    g.wait_ge(sem.sc2, 1)
    stage((2, 3), scaled, land, sem.rsa)
    g.wait_ge(sem.sc3, 1)
    stage((4, 5), scaled, land, sem.rsb)
    g.wait_ge(sem.sc4, 1)
    stage((6,), scaled, land, sem.rsd)
    stage((7,), scaled, land, sem.rse)
    g.wait_ge(sem.wdone, 1)
    stage((4, 5), own, own, sem.aga, more=[(X, up, own(0), T.XW[:], sem.xw)])
    stage((6, 7), own, own, sem.agp)
    stage((2,), own, own, sem.agb)
    g.sem_inc(sem.agi, 1)

    nq = [0]
    add, mul = AluOpType.add, AluOpType.mult

    def after(make, done):
        if nq[0]:
            v.wait_ge(sem.vq, nq[0])
        ins = make()
        if done is None:
            ins.then_inc(sem.vq, 1)
            nq[0] += 1
        else:
            ins.then_inc(done, 1)

    def tt(out, a, b, done=None):
        after(lambda: v.tensor_tensor(out, a, b, add), done)

    def ts(out, a, c, done=None):
        after(lambda: v.tensor_scalar(out, a, c, None, mul), done)

    A, H1, Q, U = T.P[:, cols(0)], T.P[:, cols(1)], T.P[:, cols(2)], T.P[:, cols(3)]
    Qq, Uq = T.P[:, 2 * F:2 * F + QW], T.P[:, 3 * F:3 * F + QW]
    v.memset(T.L[:, 0:QW], 0.0).then_inc(sem.vmem, 1)
    v.wait_ge(sem.vmem, 1)
    v.wait_ge(sem.ld2, 16)
    ts(T.S[:, cols(0, 2)], T.G[:, cols(first[2], 2)], -LR, sem.sc2)
    v.wait_ge(sem.ld3, 16)
    ts(T.S[:, cols(2, 2)], T.G[:, cols(first[4], 2)], -LR, sem.sc3)
    ts(T.S[:, cols(4, 2)], T.G[:, cols(first[6], 2)], -LR, sem.sc4)
    v.wait_ge(sem.ldO, 16)
    ts(T.SO[:], T.G[:, cols(r)], -LR)
    v.wait_ge(sem.ldM, 16)
    ts(A, T.M[:], -LR * BETA)
    tt(T.Z0[:], A, T.SO[:])
    v.wait_ge(sem.rs1, ne)
    ts(H1, land(1), -LR)
    tt(T.Z1[:], H1, T.Z0[:])
    v.wait_ge(sem.ldW, 16)
    tt(Q, T.Z1[:], T.W[:])
    for s, ks in ((sem.rsa, (2, 3)), (sem.rsb, (4, 5)), (sem.rsd, (6,))):
        v.wait_ge(s, ne)
        for k in ks:
            tt(Q, Q, land(k))
    v.wait_ge(sem.rsx, nx)
    ts(T.HX[:], T.LX[:], -LR)
    tt(Qq, Qq, T.HX[:])
    v.wait_ge(sem.rse, ne)
    tt(T.Y[:, cols(r)], Q, land(7), sem.wdone)
    tt(T.T3[:], T.L[:, cols(1, 3)], T.L[:, cols(4, 3)])
    tt(U, T.T3[:, cols(0)], T.T3[:, cols(1)])
    tt(U, U, T.T3[:, cols(2)])
    tt(U, U, T.Z1[:])
    tt(Uq, Uq, T.HX[:])
    ts(T.MO[:], U, -1.0 / LR, sem.mdone)

    g.scalar.wait_ge(sem.wdone, 1)
    g.scalar.wait_ge(sem.agi, 1)
    g.scalar.dma_start(out=T.y[:, cols(r)], in_=T.Y[:, cols(r)]).then_inc(sem.stO, 16)
    g.scalar.wait_ge(sem.mdone, 1)
    g.scalar.dma_start(out=T.mo[:], in_=T.MO[:]).then_inc(sem.stM, 16)
    g.scalar.wait_ge(sem.agc, nx)
    g.scalar.dma_start(out=T.y[:, cols(r ^ 1)], in_=T.Y[:, cols(r ^ 1)]).then_inc(sem.stL, 16)
    g.scalar.wait_ge(sem.agd, nx)
    g.scalar.dma_start(out=T.y[:, cols(r ^ 3)], in_=T.Y[:, cols(r ^ 3)]).then_inc(sem.stR, 16)
    g.sync.wait_ge(sem.aga, ne)
    g.sync.dma_start(out=T.y[:, cols(first[4], 2)], in_=T.Y[:, cols(first[4], 2)]).then_inc(sem.stH, 16)
    g.sync.wait_ge(sem.agp, ne)
    g.sync.dma_start(out=T.y[:, cols(first[6], 2)], in_=T.Y[:, cols(first[6], 2)]).then_inc(sem.stP, 16)
    g.sync.wait_ge(sem.agb, ne)
    g.sync.dma_start(out=T.y[:, cols(r ^ 2)], in_=T.Y[:, cols(r ^ 2)]).then_inc(sem.stQ, 16)

    g.wait_ge(sem.sent, sent[0])
    g.scalar.wait_ge(sem.stO, 16)
    g.scalar.wait_ge(sem.stM, 16)
    g.scalar.wait_ge(sem.stL, 16)
    g.scalar.wait_ge(sem.stR, 16)
    g.sync.wait_ge(sem.stH, 16)
    g.sync.wait_ge(sem.stP, 16)
    g.sync.wait_ge(sem.stQ, 16)
